import numpy as np
import ml_dtypes


def mxq(x, axis, fmt="e4m3"):
    dtype, down = {"e4m3": (ml_dtypes.float8_e4m3fn, 7), "e5m2": (ml_dtypes.float8_e5m2, 14)}[fmt]
    v = np.moveaxis(np.asarray(x, np.float32).astype(ml_dtypes.bfloat16).astype(np.float64), axis, -1)
    blocks = v.reshape(v.shape[:-1] + (-1, 32))
    amax = np.abs(blocks).max(-1, keepdims=True)
    byte = np.maximum(np.where(amax > 0, np.frexp(amax)[1] - 1 + 127, 0) - down, 1)
    scale = np.exp2(byte - 127.0)
    codes = (blocks / scale).astype(np.float32).astype(dtype).astype(np.float64)
    return np.moveaxis((codes * scale).reshape(v.shape), -1, axis)


WIDE = False


def mx_kscale(k):
    if not WIDE:
        return np.ones(k)
    levels = np.array([10, -10, 5, -5, 0])
    if k % 512:
        return np.exp2(np.random.permutation(np.resize(levels, k // 32))).repeat(32)
    a = np.empty((k // 512, 16))
    for p in range(k // 512):
        a[p, :8] = np.random.permutation(np.resize(levels, 8))
        for g in range(8):
            far = levels[np.abs(levels - a[p, g]) >= 10]
            a[p, g + 8] = far[np.random.randint(len(far))]
    return np.exp2(a.ravel()).repeat(32)


def f64(x):
    return np.asarray(x).astype(np.float64)


def striped(idx):
    return np.tile(np.asarray(idx).reshape(-1, 16).T, (8, 1)).astype(np.uint16)


def unstriped(offs):
    return offs[:16].T.reshape(-1).astype(np.int64)


E2M1 = np.array([0.0, 0.5, 1.0, 1.5, 2.0, 3.0, 4.0, 6.0, -0.0, -0.5, -1.0, -1.5, -2.0, -3.0, -4.0, -6.0])


def pack_weight(w, fmt):
    k, n = w.shape
    w = f64(np.asarray(w, np.float32).astype(ml_dtypes.bfloat16)).reshape(k // 32, 32, n)
    amax = np.abs(w).max(1)
    if fmt == "e4m3":
        byte = np.frexp(amax)[1] - 1 + 127 - 7
    else:
        mant, ex = np.frexp(amax / 6.0)
        byte = np.where(mant > 0.5, ex, ex - 1) + 127
    byte = np.clip(np.where(amax > 0, byte, 1), 1, 254)
    scaled = (w * np.exp2(127.0 - byte)[:, None, :]).reshape(k, n).astype(np.float32)
    by_word = np.ascontiguousarray(scaled.reshape(k // 512, 128, 4, n).transpose(0, 1, 3, 2))
    if fmt == "e4m3":
        words = by_word.astype(ml_dtypes.float8_e4m3fn).view(np.uint8)
    else:
        c = by_word.astype(ml_dtypes.float4_e2m1fn).view(np.uint8) & 0xF
        words = (c[..., 0::2] | (c[..., 1::2] << 4)).reshape(k // 512, 128, 2 * n)
    return np.ascontiguousarray(words), np.ascontiguousarray(byte.astype(np.uint8).reshape(k // 512, 16, n))


def unpack_weight(words, scales, fmt):
    g, _, n = scales.shape
    words = np.ascontiguousarray(words).reshape(g, 128, n, -1)
    if fmt == "e4m3":
        vals = words.view(ml_dtypes.float8_e4m3fn).astype(np.float64)
    else:
        nib = np.empty((g, 128, n, 4), np.uint8)
        nib[..., 0::2] = words & 0xF
        nib[..., 1::2] = words >> 4
        vals = E2M1[nib]
    vals = vals * np.repeat(np.exp2(scales.astype(np.float64) - 127.0), 8, axis=1)[..., None]
    return vals.transpose(0, 1, 3, 2).reshape(g * 512, n)


def softplus(v):
    return np.log(1.0 + np.exp(v))


def sigmoid(v):
    return 1.0 / (1.0 + np.exp(-v))


D, T, U, I, J, G = 512, 1024, 1024, 256, 512, 64


def setup_inputs():
    n = np.random.standard_normal
    idx = np.random.permutation(T)[:I]
    idx2 = np.random.permutation(U)[:J]
    fd = mx_kscale(D)
    fj = mx_kscale(J)
    tj = np.ones(U)
    tj[idx2] = fj
    tabbp = pack_weight(n((D, U)) / fd[:, None], "e2m1")
    return {
        "taba": (n((D, T)) * 1 / np.sqrt(D) * fd[:, None]).astype(np.float32),
        "tabb_words": tabbp[0],
        "tabb_scales": tabbp[1],
        "reserve": (np.random.uniform(20.0, 100.0, (I, 1))).astype(np.float32),
        "stake": (n((I, G)) * 1.5).astype(np.float32),
        "js": (np.random.uniform(4.0, 16.0, (1, J)) * fj).astype(np.float32),
        "brows": (n((D, U)) / tj).astype(np.float32),
        "old": (n((D, T)) * 2.0).astype(np.float32),
        "fade": (np.random.uniform(0.5, 1.0, (1, T))).astype(np.float32),
        "offs": striped(idx),
        "offs2": striped(idx2),
    }


def reference(taba, tabb_words, tabb_scales, reserve, stake, js, brows, old, fade, offs, offs2):
    idx = unstriped(offs)
    idx2 = unstriped(offs2)
    tabbu = unpack_weight(tabb_words, tabb_scales, "e2m1")
    tabaidxq = mxq(f64(taba)[:, idx], 0, "e4m3")
    tabbidx2g = tabbu[:, idx2]
    s = tabaidxq.T @ tabbidx2g
    p = softplus(s)
    z = np.sum(p, axis=1, keepdims=True) + f64(reserve)
    s1g = p.reshape(I, G, J // G).sum(axis=2) / z
    ds1g = f64(stake) / (s1g * 64.0 + 1.0) * 64.0
    e1 = ds1g / z
    r1 = np.repeat(e1, J // G, axis=1)
    dz = np.sum(ds1g * p.reshape(I, G, J // G).sum(axis=2) / np.square(z) * (-1.0), axis=1, keepdims=True)
    dp = r1 + dz
    ds = dp * sigmoid(s)
    gs = ds * f64(js)
    gt1 = gs.T
    bt = f64(brows)[:, idx2].T
    btq = mxq(bt, 0, "e4m3")
    gt1q = mxq(gt1, 0, "e4m3")
    gx1 = btq.T @ gt1q
    gf = np.zeros((D, T))
    gf[:, idx] = gx1
    y = f64(old) * f64(fade) + gf
    return y

@@ -1,0 +1,257 @@
+from contextlib import ExitStack
+
+import concourse.mybir as mybir
+from concourse.masks import make_identity
+
+D, T, U, I, J, G = 512, 1024, 1024, 256, 512, 64
+FLOPS = 2 * D * I * J * 2
+
+F32 = mybir.dt.float32
+BF16 = mybir.dt.bfloat16
+I32 = mybir.dt.int32
+U32 = mybir.dt.uint32
+U16 = mybir.dt.uint16
+U8 = mybir.dt.uint8
+FP8X4 = mybir.dt.float8_e4m3fn_x4
+FP4X4 = mybir.dt.float4_e2m1fn_x4
+ALU = mybir.AluOpType
+ACT = mybir.ActivationFunctionType
+AXIS = mybir.AxisListType
+
+P = 128
+PACK = 4
+HALVES = I // P
+PLANES = D // P
+TBLOCKS = T // P
+GROUP = J // G
+BANK = 512
+TINY = 2.0 ** -60
+FADE_ROW, JS_ROW, RESERVE_ROW = 0, 64, 96
+
+
+def tile_attend_bpairquota_x_kernel(tc, taba, tabb_words, tabb_scales, reserve, stake, js, brows, old, fade, offs, offs2, out):
+    nc = tc.nc
+    with ExitStack() as ctx:
+        lists = ctx.enter_context(tc.tile_pool(name="lists", bufs=1))
+        sb = ctx.enter_context(tc.tile_pool(name="sb", bufs=1))
+        ps = ctx.enter_context(tc.psum_pool(name="ps", bufs=1))
+
+        def bank(n, name):
+            return ps.tile([P, BANK], F32, name=name, tag="bank%d" % n)
+
+        scale_table = sb.tile([P, U], U8, name="scale_table")
+        vector_rows = sb.tile([P, P], F32, name="vector_rows")
+        placed = [sb.tile([P, T], F32, name="placed%d" % m) for m in range(PLANES)]
+        ident = sb.tile([P, P], F32, name="ident")
+        make_identity(nc, ident[:])
+
+        list_b = lists.tile([P, J // 16], U16, name="list_b")
+        nc.sync.dma_start(list_b[:], offs2)
+        for q in range(4):
+            nc.scalar.dma_start(scale_table[32 * q : 32 * q + 32, :].bitcast(I32), tabb_scales[:, 4 * q : 4 * q + 4, :].bitcast(I32).to_broadcast([8, 4, U // 4]))
+        warm = sb.tile([P, 8], F32, name="warm")
+        nc.vector.memset(warm[:], 0.0)
+        warm_out = sb.tile([P, 8], F32, name="warm_out")
+        nc.scalar.activation(warm_out[:], warm[:], ACT.Sigmoid)
+        for m in range(PLANES):
+            (nc.vector if m < 2 else nc.gpsimd).memset(placed[m][:], 0.0)
+        word_table = sb.tile([P, U], U16, name="word_table")
+        nc.sync.dma_start(word_table[:].bitcast(I32), tabb_words[0].bitcast(I32))
+        list_a = lists.tile([P, I // 16], U16, name="list_a")
+        nc.sync.dma_start(list_a[:], offs)
+        a_rows = taba.rearrange("(p r) t -> p r t", r=PACK)
+        a_table = [sb.tile([P, T], F32, name="a_table%d" % r) for r in range(PACK)]
+        for r in range(PACK):
+            nc.sync.dma_start(a_table[r][:], a_rows[:, r, :])
+        nc.sync.dma_start(vector_rows[FADE_ROW:JS_ROW, :], fade.rearrange("o (b p) -> o b p", p=P).to_broadcast([8, TBLOCKS, P]))
+        nc.sync.dma_start(vector_rows[JS_ROW:RESERVE_ROW, :], js.rearrange("o (b p) -> o b p", p=P).to_broadcast([8, J // P, P]))
+        nc.sync.dma_start(vector_rows[RESERVE_ROW:P, :], reserve.rearrange("(a p) o -> o a p", p=P).to_broadcast([16, HALVES, P]))
+        b_table = [sb.tile([P, U], F32, name="b_table%d" % m, tag="b_table%d" % m) for m in range(PLANES)]
+        nc.sync.dma_start(b_table[0][:], brows[0:P, :])
+        stakes = sb.tile([P, HALVES, G], F32, name="stakes")
+        nc.sync.dma_start(stakes[:], stake.rearrange("(a p) g -> p a g", p=P))
+        for m in range(1, PLANES):
+            nc.sync.dma_start(b_table[m][:], brows[m * P : (m + 1) * P, :])
+        old_half = [sb.tile([P, PLANES, BANK], F32, name="old_half%d" % h) for h in range(2)]
+        for h in range(2):
+            nc.sync.dma_start(old_half[h][:], old[:, h * BANK : (h + 1) * BANK].rearrange("(m p) t -> p m t", p=P))
+
+        b_scales = sb.tile([P, J], U8, name="b_scales", align_bytes=64)
+        nc.vector.tensor_copy(b_scales[:], scale_table[:].indirect(list_b[:]))
+        b_words = sb.tile([P, J], U16, name="b_words", align_bytes=64)
+        nc.vector.tensor_copy(b_words[:], word_table[:].indirect(list_b[:]))
+        a_woven = sb.tile([P, I, PACK], BF16, name="a_woven", align_bytes=64)
+        for r in range(PACK):
+            nc.vector.tensor_copy(a_woven[:, :, r], a_table[r][:].indirect(list_a[:]))
+        a_codes = sb.tile([P, I], U32, name="a_codes", align_bytes=64)
+        a_scales = sb.tile([P, I], U8, name="a_scales", align_bytes=64)
+        nc.vector.quantize_mx(out=a_codes[:].bitcast(FP8X4), scales=a_scales[:], in_=a_woven[:].rearrange("p i r -> p (i r)"))
+
+        turned = bank(2, "turned")
+        nc.tensor.transpose(turned[:, 0:P], vector_rows[:], ident[:])
+        columns = sb.tile([P, P], F32, name="columns")
+        nc.scalar.copy(columns[:], turned[:, 0:P])
+        js_wide = bank(3, "js_wide")
+        for b in range(J // P):
+            nc.tensor.transpose(js_wide[:, b * P : (b + 1) * P], columns[:, JS_ROW + b : JS_ROW + b + 1].to_broadcast([P, P]), ident[:])
+
+        score = [bank(a, "score%d" % a) for a in range(HALVES)]
+        for a in range(HALVES):
+            nc.tensor.matmul_mx(out=score[a][:], lhsT=a_codes[:, a * P : (a + 1) * P].bitcast(FP8X4), lhsT_scale=a_scales[:, a * P : (a + 1) * P],
+                                rhs=b_words[:].bitcast(FP4X4), rhs_scale=b_scales[:], start=True, stop=True)
+        low = [sb.tile([P, J], F32, name="low%d" % a, tag="low%d" % a, align_bytes=64) for a in range(HALVES)]
+        sig = [sb.tile([P, J], F32, name="sig%d" % a) for a in range(HALVES)]
+        log_low = [sb.tile([P, J], F32, name="log_low%d" % a) for a in range(HALVES)]
+        for a in range(HALVES):
+            nc.scalar.activation(low[a][:], score[a][:], ACT.Sigmoid, scale=-1.0)
+            nc.scalar.activation(sig[a][:], score[a][:], ACT.Sigmoid)
+        for a in range(HALVES):
+            nc.scalar.activation(log_low[a][:], low[a][:], ACT.Ln, bias=TINY)
+
+        bt_woven = sb.tile([P, D, PACK], BF16, name="bt_woven", tag="low1", align_bytes=64)
+        bt_codes = sb.tile([P, D], U32, name="bt_codes", align_bytes=64)
+        bt_scales = sb.tile([P, D], U8, name="bt_scales", align_bytes=64)
+        for pair in range(PLANES // 2):
+            bt_turned = bank(4 + pair, "bt_turned%d" % pair)
+            for k in range(2):
+                m = 2 * pair + k
+                b_picked = sb.tile([P, J], BF16, name="b_picked%d" % m)
+                nc.vector.tensor_copy(b_picked[:], b_table[m][:].indirect(list_b[:]))
+                words = b_picked[:].bitcast(F32)
+                for u in range(2):
+                    nc.tensor.transpose(bt_turned[:, (2 * k + u) * P : (2 * k + u + 1) * P], words[:, u : J // 2 : 2], ident[:])
+            nc.scalar.copy(bt_woven[:, pair * 2 * P : (pair + 1) * 2 * P, :].bitcast(F32).rearrange("p (k d) u -> p k d u", k=2),
+                           bt_turned[:].rearrange("p (k u d) -> p k d u", k=2, u=2))
+
+        faded = sb.tile([P, TBLOCKS, D], F32, name="faded")
+        for b in range(TBLOCKS):
+            old_turned = bank((6, 7, 2)[b % 3], "old_turned%d" % b)
+            h, c = divmod(b, TBLOCKS // 2)
+            for m in range(PLANES):
+                nc.tensor.transpose(old_turned[:, m * P : (m + 1) * P], old_half[h][:, m, c * P : (c + 1) * P], ident[:])
+            nc.scalar.activation(faded[:, b, :], old_turned[:], ACT.Copy, scale=columns[:, FADE_ROW + b : FADE_ROW + b + 1])
+
+        sig_js = [sb.tile([P, J], F32, name="sig_js%d" % a, tag="b_table%d" % (2 + a)) for a in range(HALVES)]
+        soft = [sb.tile([P, J], F32, name="soft%d" % a) for a in range(HALVES)]
+        row_sum = [sb.tile([P, 1], F32, name="row_sum%d" % a) for a in range(HALVES)]
+        group_sum = [sb.tile([P, G], F32, name="group_sum%d" % a) for a in range(HALVES)]
+        den = [sb.tile([P, G + 1], F32, name="den%d" % a) for a in range(HALVES)]
+        inv = [sb.tile([P, G + 1], F32, name="inv%d" % a) for a in range(HALVES)]
+        e1 = [sb.tile([P, G, 1], F32, name="e1_%d" % a) for a in range(HALVES)]
+        staked = [sb.tile([P, G], F32, name="staked%d" % a) for a in range(HALVES)]
+        terms = [sb.tile([P, G], F32, name="terms%d" % a) for a in range(HALVES)]
+        minus_dz = [sb.tile([P, 1], F32, name="minus_dz%d" % a) for a in range(HALVES)]
+        gs = [sb.tile([P, J], BF16, name="gs%d" % a) for a in range(HALVES)]
+        gt_codes = sb.tile([P, I], U32, name="gt_codes", align_bytes=64)
+        gt_scales = sb.tile([P, I], U8, name="gt_scales", align_bytes=64)
+        gt_woven = [sb.tile([P, P, PACK], BF16, name="gt_woven%d" % a, align_bytes=64) for a in range(HALVES)]
+
+        for a in range(HALVES):
+            nc.vector.tensor_tensor(sig_js[a][:], sig[a][:], js_wide[:], ALU.mult)
+
+        def softplus(a):
+            nc.vector.scalar_tensor_tensor(soft[a][:], log_low[a][:], -1.0, score[a][:], ALU.mult, ALU.max, accum_out=row_sum[a][:])
+
+        def sums(a):
+            nc.vector.tensor_reduce(group_sum[a][:], soft[a][:].rearrange("p (g k) -> p g k", k=GROUP), AXIS.X, ALU.add)
+            nc.vector.tensor_scalar(den[a][:, G : G + 1], row_sum[a][:], columns[:, RESERVE_ROW + a : RESERVE_ROW + a + 1], None, ALU.add)
+
+        def denominators(a):
+            nc.vector.tensor_scalar(den[a][:, 0:G], group_sum[a][:], 64.0, den[a][:, G : G + 1], ALU.mult, ALU.add)
+            nc.vector.scalar_tensor_tensor(staked[a][:], group_sum[a][:], 64.0, stakes[:, a, :], ALU.mult, ALU.mult)
+
+        def inverses(a):
+            nc.vector.reciprocal(inv[a][:], den[a][:])
+
+        def group_terms(a):
+            nc.vector.scalar_tensor_tensor(e1[a][:, :, 0], inv[a][:, 0:G], 64.0, stakes[:, a, :], ALU.mult, ALU.mult)
+
+        def row_term(a):
+            nc.vector.scalar_tensor_tensor(terms[a][:], inv[a][:, 0:G], inv[a][:, G : G + 1], staked[a][:], ALU.mult, ALU.mult, accum_out=minus_dz[a][:])
+
+        def gradient(a):
+            nc.vector.scalar_tensor_tensor(gs[a][:].rearrange("p (g k) -> p g k", k=GROUP), e1[a][:].to_broadcast([P, G, GROUP]), minus_dz[a][:],
+                                           sig_js[a][:].rearrange("p (g k) -> p g k", k=GROUP), ALU.subtract, ALU.mult)
+            gt_turned = bank(7 - a, "gt_turned%d" % a)
+            words = gs[a][:].bitcast(F32)
+            for u in range(2):
+                nc.tensor.transpose(gt_turned[:, u * P : (u + 1) * P], words[:, u : J // 2 : 2], ident[:])
+            nc.scalar.copy(gt_woven[a][:].bitcast(F32), gt_turned[:, 0 : 2 * P].rearrange("p (u i) -> p i u", u=2))
+
+        softplus(0)
+        sums(0)
+        softplus(1)
+        denominators(0)
+        sums(1)
+        inverses(0)
+        denominators(1)
+        row_term(0)
+        group_terms(0)
+        inverses(1)
+        gradient(0)
+        row_term(1)
+        group_terms(1)
+        nc.vector.quantize_mx(out=bt_codes[:].bitcast(FP8X4), scales=bt_scales[:], in_=bt_woven[:].rearrange("p d r -> p (d r)"))
+        gradient(1)
+
+        def product(name, n, planes, i0, i1):
+            width = i1 - i0
+            acc = bank(n, name)
+            for k, m in enumerate(planes):
+                nc.tensor.matmul_mx(out=acc[:, k * width : (k + 1) * width], lhsT=bt_codes[:, m * P : (m + 1) * P].bitcast(FP8X4), lhsT_scale=bt_scales[:, m * P : (m + 1) * P],
+                                    rhs=gt_codes[:, i0:i1].bitcast(FP8X4), rhs_scale=gt_scales[:, i0:i1], start=True, stop=True)
+            gx = sb.tile([P, len(planes), width], F32, name=name + "_sb")
+            nc.scalar.copy(gx[:].rearrange("p m i -> p (m i)"), acc[:, 0 : len(planes) * width])
+            return gx
+
+        def scatter(m, i0, i1, values):
+            nc.vector.tensor_copy(placed[m][:].indirect(list_a[:, i0 // 16 : i1 // 16]), values)
+
+        gx_front = []
+        for a in range(HALVES):
+            nc.vector.quantize_mx(out=gt_codes[:, a * P : (a + 1) * P].bitcast(FP8X4), scales=gt_scales[:, a * P : (a + 1) * P], in_=gt_woven[a][:].rearrange("p i r -> p (i r)"))
+            gx_front.append(product("front%d" % a, a, (0, 1), a * P, (a + 1) * P))
+        gx_rear = product("rear", 4, (2, 3), 0, I)
+
+        result = [sb.tile([P, T], F32, name="result%d" % m) for m in range(PLANES)]
+
+        def store(queue, m, c0, c1):
+            queue.dma_start(out[m * P : (m + 1) * P, c0:c1], result[m][:, c0:c1])
+
+        def add_on_vector(m, pieces):
+            for h in range(2):
+                back = bank((6, 7, 1, 4)[2 * (m - 2) + h], "back%d_%d" % (m, h))
+                for c in range(TBLOCKS // 2):
+                    nc.tensor.transpose(back[:, c * P : (c + 1) * P], faded[:, h * (TBLOCKS // 2) + c, m * P : (m + 1) * P], ident[:])
+                width = BANK // pieces[h]
+                for c0 in range(0, BANK, width):
+                    t0 = h * BANK + c0
+                    nc.vector.tensor_tensor(result[m][:, t0 : t0 + width], back[:, c0 : c0 + width], placed[m][:, t0 : t0 + width], ALU.add)
+                    store(nc.sync, m, t0, t0 + width)
+
+        def add_on_tensor(m):
+            placed_turned = sb.tile([P, TBLOCKS, P], F32, name="placed_turned%d" % m)
+            for h in range(2):
+                forth = bank((2, 3)[h], "forth%d_%d" % (m, h))
+                for c in range(TBLOCKS // 2):
+                    b = h * (TBLOCKS // 2) + c
+                    nc.tensor.transpose(forth[:, c * P : (c + 1) * P], placed[m][:, b * P : (b + 1) * P], ident[:])
+                nc.scalar.copy(placed_turned[:, h * (TBLOCKS // 2) : (h + 1) * (TBLOCKS // 2), :].rearrange("p c d -> p (c d)"), forth[:])
+            for h in range(2):
+                back = bank((5, 0)[h], "sum%d_%d" % (m, h))
+                for c in range(TBLOCKS // 2):
+                    b = h * (TBLOCKS // 2) + c
+                    nc.tensor.matmul(back[:, c * P : (c + 1) * P], faded[:, b, m * P : (m + 1) * P], ident[:], start=True, stop=False, is_transpose=True)
+                    nc.tensor.matmul(back[:, c * P : (c + 1) * P], placed_turned[:, b, :], ident[:], start=False, stop=True, is_transpose=True)
+                nc.scalar.copy(result[m][:, h * BANK : (h + 1) * BANK], back[:])
+                store(nc.scalar, m, h * BANK, (h + 1) * BANK)
+
+        for a in range(HALVES):
+            for m in range(2):
+                scatter(m, a * P, (a + 1) * P, gx_front[a][:, m, :])
+        add_on_tensor(0)
+        scatter(2, 0, I, gx_rear[:, 0, :])
+        add_on_tensor(1)
+        add_on_vector(2, (1, 1))
+        scatter(3, 0, I, gx_rear[:, 1, :])
+        add_on_vector(3, (1, 2))

@@ -53,8 +53,13 @@ def tile_attend_bpairquota_x_kernel(tc, taba, tabb_words, tabb_scales, reserve, 
         nc.vector.memset(warm[:], 0.0)
         warm_out = sb.tile([P, 8], F32, name="warm_out")
         nc.scalar.activation(warm_out[:], warm[:], ACT.Sigmoid)
+        nc.gpsimd.dma_start(vector_rows[FADE_ROW:JS_ROW, :], fade.rearrange("o (b p) -> o b p", p=P).to_broadcast([8, TBLOCKS, P]))
+        nc.gpsimd.dma_start(vector_rows[JS_ROW:RESERVE_ROW, :], js.rearrange("o (b p) -> o b p", p=P).to_broadcast([8, J // P, P]))
+        nc.gpsimd.dma_start(vector_rows[RESERVE_ROW:P, :], reserve.rearrange("(a p) o -> o a p", p=P).to_broadcast([16, HALVES, P]))
+        stakes = sb.tile([P, HALVES, G], F32, name="stakes")
+        nc.gpsimd.dma_start(stakes[:], stake.rearrange("(a p) g -> p a g", p=P))
         for m in range(PLANES):
-            (nc.vector if m < 2 else nc.gpsimd).memset(placed[m][:], 0.0)
+            (nc.vector if m < 2 else nc.gpsimd).memset(placed[m][:].bitcast(I32), 0)
         word_table = sb.tile([P, U], U16, name="word_table")
         nc.sync.dma_start(word_table[:].bitcast(I32), tabb_words[0].bitcast(I32))
         list_a = lists.tile([P, I // 16], U16, name="list_a")
@@ -63,13 +68,8 @@ def tile_attend_bpairquota_x_kernel(tc, taba, tabb_words, tabb_scales, reserve, 
         a_table = [sb.tile([P, T], F32, name="a_table%d" % r) for r in range(PACK)]
         for r in range(PACK):
             nc.sync.dma_start(a_table[r][:], a_rows[:, r, :])
-        nc.sync.dma_start(vector_rows[FADE_ROW:JS_ROW, :], fade.rearrange("o (b p) -> o b p", p=P).to_broadcast([8, TBLOCKS, P]))
-        nc.sync.dma_start(vector_rows[JS_ROW:RESERVE_ROW, :], js.rearrange("o (b p) -> o b p", p=P).to_broadcast([8, J // P, P]))
-        nc.sync.dma_start(vector_rows[RESERVE_ROW:P, :], reserve.rearrange("(a p) o -> o a p", p=P).to_broadcast([16, HALVES, P]))
         b_table = [sb.tile([P, U], F32, name="b_table%d" % m, tag="b_table%d" % m) for m in range(PLANES)]
         nc.sync.dma_start(b_table[0][:], brows[0:P, :])
-        stakes = sb.tile([P, HALVES, G], F32, name="stakes")
-        nc.sync.dma_start(stakes[:], stake.rearrange("(a p) g -> p a g", p=P))
         for m in range(1, PLANES):
             nc.sync.dma_start(b_table[m][:], brows[m * P : (m + 1) * P, :])
         old_half = [sb.tile([P, PLANES, BANK], F32, name="old_half%d" % h) for h in range(2)]
@@ -81,11 +81,27 @@ def tile_attend_bpairquota_x_kernel(tc, taba, tabb_words, tabb_scales, reserve, 
         b_words = sb.tile([P, J], U16, name="b_words", align_bytes=64)
         nc.vector.tensor_copy(b_words[:], word_table[:].indirect(list_b[:]))
         a_woven = sb.tile([P, I, PACK], BF16, name="a_woven", align_bytes=64)
-        for r in range(PACK):
+        a_picked = sb.tile([P, 2, I], BF16, name="a_picked")
+        for r in range(2):
+            nc.vector.tensor_copy(a_picked[:, r, :], a_table[r][:].indirect(list_a[:]))
+        nc.scalar.copy(a_woven[:, :, 0:2], a_picked[:].rearrange("p r i -> p i r"))
+        for r in range(2, PACK):
             nc.vector.tensor_copy(a_woven[:, :, r], a_table[r][:].indirect(list_a[:]))
         a_codes = sb.tile([P, I], U32, name="a_codes", align_bytes=64)
         a_scales = sb.tile([P, I], U8, name="a_scales", align_bytes=64)
         nc.vector.quantize_mx(out=a_codes[:].bitcast(FP8X4), scales=a_scales[:], in_=a_woven[:].rearrange("p i r -> p (i r)"))
+
+        score = [bank(a, "score%d" % a) for a in range(HALVES)]
+        for a in range(HALVES):
+            nc.tensor.matmul_mx(out=score[a][:], lhsT=a_codes[:, a * P : (a + 1) * P].bitcast(FP8X4), lhsT_scale=a_scales[:, a * P : (a + 1) * P],
+                                rhs=b_words[:].bitcast(FP4X4), rhs_scale=b_scales[:], start=True, stop=True)
+        low = [sb.tile([P, J], F32, name="low%d" % a, tag="low%d" % a, align_bytes=64) for a in range(HALVES)]
+        sig = [sb.tile([P, J], F32, name="sig%d" % a, tag="low%d" % a, align_bytes=64) for a in range(HALVES)]
+        log_low = [sb.tile([P, J], F32, name="log_low%d" % a, tag="log_low%d" % a, align_bytes=64) for a in range(HALVES)]
+        for a in range(HALVES):
+            nc.scalar.activation(low[a][:], score[a][:], ACT.Sigmoid, scale=-1.0)
+        for a in range(HALVES):
+            nc.scalar.activation(log_low[a][:], low[a][:], ACT.Ln, bias=TINY)
 
         turned = bank(2, "turned")
         nc.tensor.transpose(turned[:, 0:P], vector_rows[:], ident[:])
@@ -95,50 +111,27 @@ def tile_attend_bpairquota_x_kernel(tc, taba, tabb_words, tabb_scales, reserve, 
         for b in range(J // P):
             nc.tensor.transpose(js_wide[:, b * P : (b + 1) * P], columns[:, JS_ROW + b : JS_ROW + b + 1].to_broadcast([P, P]), ident[:])
 
-        score = [bank(a, "score%d" % a) for a in range(HALVES)]
-        for a in range(HALVES):
-            nc.tensor.matmul_mx(out=score[a][:], lhsT=a_codes[:, a * P : (a + 1) * P].bitcast(FP8X4), lhsT_scale=a_scales[:, a * P : (a + 1) * P],
-                                rhs=b_words[:].bitcast(FP4X4), rhs_scale=b_scales[:], start=True, stop=True)
-        low = [sb.tile([P, J], F32, name="low%d" % a, tag="low%d" % a, align_bytes=64) for a in range(HALVES)]
-        sig = [sb.tile([P, J], F32, name="sig%d" % a) for a in range(HALVES)]
-        log_low = [sb.tile([P, J], F32, name="log_low%d" % a) for a in range(HALVES)]
-        for a in range(HALVES):
-            nc.scalar.activation(low[a][:], score[a][:], ACT.Sigmoid, scale=-1.0)
-            nc.scalar.activation(sig[a][:], score[a][:], ACT.Sigmoid)
-        for a in range(HALVES):
-            nc.scalar.activation(log_low[a][:], low[a][:], ACT.Ln, bias=TINY)
-
-        bt_woven = sb.tile([P, D, PACK], BF16, name="bt_woven", tag="low1", align_bytes=64)
-        bt_codes = sb.tile([P, D], U32, name="bt_codes", align_bytes=64)
+        bt_woven = sb.tile([P, D, PACK], BF16, name="bt_woven", tag="log_low1", align_bytes=64)
         bt_scales = sb.tile([P, D], U8, name="bt_scales", align_bytes=64)
+        bt_turned = [bank(4 + pair, "bt_turned%d" % pair) for pair in range(PLANES // 2)]
         for pair in range(PLANES // 2):
-            bt_turned = bank(4 + pair, "bt_turned%d" % pair)
             for k in range(2):
                 m = 2 * pair + k
                 b_picked = sb.tile([P, J], BF16, name="b_picked%d" % m)
                 nc.vector.tensor_copy(b_picked[:], b_table[m][:].indirect(list_b[:]))
                 words = b_picked[:].bitcast(F32)
                 for u in range(2):
-                    nc.tensor.transpose(bt_turned[:, (2 * k + u) * P : (2 * k + u + 1) * P], words[:, u : J // 2 : 2], ident[:])
-            nc.scalar.copy(bt_woven[:, pair * 2 * P : (pair + 1) * 2 * P, :].bitcast(F32).rearrange("p (k d) u -> p k d u", k=2),
-                           bt_turned[:].rearrange("p (k u d) -> p k d u", k=2, u=2))
+                    nc.tensor.transpose(bt_turned[pair][:, (2 * k + u) * P : (2 * k + u + 1) * P], words[:, u : J // 2 : 2], ident[:])
 
-        faded = sb.tile([P, TBLOCKS, D], F32, name="faded")
-        for b in range(TBLOCKS):
-            old_turned = bank((6, 7, 2)[b % 3], "old_turned%d" % b)
-            h, c = divmod(b, TBLOCKS // 2)
-            for m in range(PLANES):
-                nc.tensor.transpose(old_turned[:, m * P : (m + 1) * P], old_half[h][:, m, c * P : (c + 1) * P], ident[:])
-            nc.scalar.activation(faded[:, b, :], old_turned[:], ACT.Copy, scale=columns[:, FADE_ROW + b : FADE_ROW + b + 1])
-
-        sig_js = [sb.tile([P, J], F32, name="sig_js%d" % a, tag="b_table%d" % (2 + a)) for a in range(HALVES)]
         soft = [sb.tile([P, J], F32, name="soft%d" % a) for a in range(HALVES)]
         row_sum = [sb.tile([P, 1], F32, name="row_sum%d" % a) for a in range(HALVES)]
-        group_sum = [sb.tile([P, G], F32, name="group_sum%d" % a) for a in range(HALVES)]
+        group_sum = [sb.tile([P, G], F32, name="group_sum%d" % a, tag=("sig_js", "group_sum1")[a]) for a in range(HALVES)]
+        sig_js = [sb.tile([P, J], F32, name="sig_js%d" % a, tag="sig_js") for a in range(HALVES)]
         den = [sb.tile([P, G + 1], F32, name="den%d" % a) for a in range(HALVES)]
-        inv = [sb.tile([P, G + 1], F32, name="inv%d" % a) for a in range(HALVES)]
-        e1 = [sb.tile([P, G, 1], F32, name="e1_%d" % a) for a in range(HALVES)]
-        staked = [sb.tile([P, G], F32, name="staked%d" % a) for a in range(HALVES)]
+        e1 = [sb.tile([P, G, 1], F32, name="e1_%d" % a, tag="e1_%d" % a) for a in range(HALVES)]
+        inv = [sb.tile([P, G + 1], F32, name="inv%d" % a, tag=("inv0", "e1_0")[a]) for a in range(HALVES)]
+        staked = [sb.tile([P, G], F32, name="staked%d" % a, tag="staked%d" % a, align_bytes=64) for a in range(HALVES)]
+        bt_codes = sb.tile([P, D], U32, name="bt_codes", tag="staked0", align_bytes=64)
         terms = [sb.tile([P, G], F32, name="terms%d" % a) for a in range(HALVES)]
         minus_dz = [sb.tile([P, 1], F32, name="minus_dz%d" % a) for a in range(HALVES)]
         gs = [sb.tile([P, J], BF16, name="gs%d" % a) for a in range(HALVES)]
@@ -146,7 +139,7 @@ def tile_attend_bpairquota_x_kernel(tc, taba, tabb_words, tabb_scales, reserve, 
         gt_scales = sb.tile([P, I], U8, name="gt_scales", align_bytes=64)
         gt_woven = [sb.tile([P, P, PACK], BF16, name="gt_woven%d" % a, align_bytes=64) for a in range(HALVES)]
 
-        for a in range(HALVES):
+        def scaled_sigmoid(a):
             nc.vector.tensor_tensor(sig_js[a][:], sig[a][:], js_wide[:], ALU.mult)
 
         def softplus(a):
@@ -172,46 +165,64 @@ def tile_attend_bpairquota_x_kernel(tc, taba, tabb_words, tabb_scales, reserve, 
         def gradient(a):
             nc.vector.scalar_tensor_tensor(gs[a][:].rearrange("p (g k) -> p g k", k=GROUP), e1[a][:].to_broadcast([P, G, GROUP]), minus_dz[a][:],
                                            sig_js[a][:].rearrange("p (g k) -> p g k", k=GROUP), ALU.subtract, ALU.mult)
-            gt_turned = bank(7 - a, "gt_turned%d" % a)
+            gt_turned = bank((6, 7)[a], "gt_turned%d" % a)
             words = gs[a][:].bitcast(F32)
             for u in range(2):
                 nc.tensor.transpose(gt_turned[:, u * P : (u + 1) * P], words[:, u : J // 2 : 2], ident[:])
             nc.scalar.copy(gt_woven[a][:].bitcast(F32), gt_turned[:, 0 : 2 * P].rearrange("p (u i) -> p i u", u=2))
 
-        softplus(0)
-        sums(0)
-        softplus(1)
-        denominators(0)
-        sums(1)
-        inverses(0)
-        denominators(1)
-        row_term(0)
-        group_terms(0)
-        inverses(1)
-        gradient(0)
-        row_term(1)
-        group_terms(1)
-        nc.vector.quantize_mx(out=bt_codes[:].bitcast(FP8X4), scales=bt_scales[:], in_=bt_woven[:].rearrange("p d r -> p (d r)"))
-        gradient(1)
+        faded = sb.tile([P, TBLOCKS, D], F32, name="faded")
 
-        def product(name, n, planes, i0, i1):
-            width = i1 - i0
-            acc = bank(n, name)
-            for k, m in enumerate(planes):
-                nc.tensor.matmul_mx(out=acc[:, k * width : (k + 1) * width], lhsT=bt_codes[:, m * P : (m + 1) * P].bitcast(FP8X4), lhsT_scale=bt_scales[:, m * P : (m + 1) * P],
-                                    rhs=gt_codes[:, i0:i1].bitcast(FP8X4), rhs_scale=gt_scales[:, i0:i1], start=True, stop=True)
-            gx = sb.tile([P, len(planes), width], F32, name=name + "_sb")
-            nc.scalar.copy(gx[:].rearrange("p m i -> p (m i)"), acc[:, 0 : len(planes) * width])
-            return gx
+        def fade_old(h):
+            for c in range(TBLOCKS // 2):
+                b = h * (TBLOCKS // 2) + c
+                old_turned = bank((4, 5, 0, 1)[c], "old_turned%d" % b)
+                for m in range(PLANES):
+                    nc.tensor.transpose(old_turned[:, m * P : (m + 1) * P], old_half[h][:, m, c * P : (c + 1) * P], ident[:])
+                nc.scalar.activation(faded[:, b, :], old_turned[:], ACT.Copy, scale=columns[:, FADE_ROW + b : FADE_ROW + b + 1])
 
-        def scatter(m, i0, i1, values):
-            nc.vector.tensor_copy(placed[m][:].indirect(list_a[:, i0 // 16 : i1 // 16]), values)
-
-        gx_front = []
         for a in range(HALVES):
-            nc.vector.quantize_mx(out=gt_codes[:, a * P : (a + 1) * P].bitcast(FP8X4), scales=gt_scales[:, a * P : (a + 1) * P], in_=gt_woven[a][:].rearrange("p i r -> p (i r)"))
-            gx_front.append(product("front%d" % a, a, (0, 1), a * P, (a + 1) * P))
-        gx_rear = product("rear", 4, (2, 3), 0, I)
+            softplus(a)
+        for a in range(HALVES):
+            nc.scalar.activation(sig[a][:], score[a][:], ACT.Sigmoid)
+        for pair in range(PLANES // 2):
+            nc.scalar.copy(bt_woven[:, pair * 2 * P : (pair + 1) * 2 * P, :].bitcast(F32).rearrange("p (k d) u -> p k d u", k=2),
+                           bt_turned[pair][:].rearrange("p (k u d) -> p k d u", k=2, u=2))
+        for a in range(HALVES):
+            sums(a)
+            denominators(a)
+            inverses(a)
+            row_term(a)
+            group_terms(a)
+            scaled_sigmoid(a)
+            gradient(a)
+            if a == 0:
+                nc.vector.quantize_mx(out=bt_codes[:].bitcast(FP8X4), scales=bt_scales[:], in_=bt_woven[:].rearrange("p d r -> p (d r)"))
+
+        def quantise_gt(a):
+            cols = slice(a * P, (a + 1) * P)
+            nc.vector.quantize_mx(out=gt_codes[:, cols].bitcast(FP8X4), scales=gt_scales[:, cols], in_=gt_woven[a][:].rearrange("p i r -> p (i r)"))
+
+        def second_product(a, planes, n):
+            cols = slice(a * P, (a + 1) * P)
+            product = bank(n, "product%d_%d" % (a, planes[0]))
+            for k, m in enumerate(planes):
+                nc.tensor.matmul_mx(out=product[:, k * P : (k + 1) * P], lhsT=bt_codes[:, m * P : (m + 1) * P].bitcast(FP8X4), lhsT_scale=bt_scales[:, m * P : (m + 1) * P],
+                                    rhs=gt_codes[:, cols].bitcast(FP8X4), rhs_scale=gt_scales[:, cols], start=True, stop=True)
+            return product
+
+        quantise_gt(0)
+        quantise_gt(1)
+        def place(product, k, m, a, tag):
+            values = sb.tile([P, P], F32, name="gx%d_%d" % (m, a), tag=tag)
+            nc.scalar.copy(values[:], product[:, k * P : (k + 1) * P])
+            nc.vector.tensor_copy(placed[m][:].indirect(list_a[:, a * (P // 16) : (a + 1) * (P // 16)]), values[:])
+
+        front = second_product(0, (0, 1), 2)
+        place(front, 0, 0, 0, "gx_0")
+        place(front, 1, 1, 0, "gx_1")
+        rear = second_product(0, (2, 3), 7)
+        place(rear, 0, 2, 0, "gx_2")
 
         result = [sb.tile([P, T], F32, name="result%d" % m) for m in range(PLANES)]
 
@@ -220,7 +231,7 @@ def tile_attend_bpairquota_x_kernel(tc, taba, tabb_words, tabb_scales, reserve, 
 
         def add_on_vector(m, pieces):
             for h in range(2):
-                back = bank((6, 7, 1, 4)[2 * (m - 2) + h], "back%d_%d" % (m, h))
+                back = bank((2, 3, 7, 4)[2 * (m - 2) + h], "back%d_%d" % (m, h))
                 for c in range(TBLOCKS // 2):
                     nc.tensor.transpose(back[:, c * P : (c + 1) * P], faded[:, h * (TBLOCKS // 2) + c, m * P : (m + 1) * P], ident[:])
                 width = BANK // pieces[h]
@@ -229,16 +240,27 @@ def tile_attend_bpairquota_x_kernel(tc, taba, tabb_words, tabb_scales, reserve, 
                     nc.vector.tensor_tensor(result[m][:, t0 : t0 + width], back[:, c0 : c0 + width], placed[m][:, t0 : t0 + width], ALU.add)
                     store(nc.sync, m, t0, t0 + width)
 
+        def add_on_gpsimd(m):
+            faded_plane = sb.tile([P, T], F32, name="faded_plane%d" % m)
+            for h in range(2):
+                cols = slice(h * BANK, (h + 1) * BANK)
+                back = bank((2, 3)[h], "back%d_%d" % (m, h))
+                for c in range(TBLOCKS // 2):
+                    nc.tensor.transpose(back[:, c * P : (c + 1) * P], faded[:, h * (TBLOCKS // 2) + c, m * P : (m + 1) * P], ident[:])
+                nc.scalar.copy(faded_plane[:, cols], back[:])
+                nc.gpsimd.tensor_tensor(result[m][:, cols], faded_plane[:, cols], placed[m][:, cols], ALU.add)
+                store(nc.sync, m, h * BANK, (h + 1) * BANK)
+
         def add_on_tensor(m):
             placed_turned = sb.tile([P, TBLOCKS, P], F32, name="placed_turned%d" % m)
             for h in range(2):
-                forth = bank((2, 3)[h], "forth%d_%d" % (m, h))
+                forth = bank((4, 5)[h], "forth%d_%d" % (m, h))
                 for c in range(TBLOCKS // 2):
                     b = h * (TBLOCKS // 2) + c
                     nc.tensor.transpose(forth[:, c * P : (c + 1) * P], placed[m][:, b * P : (b + 1) * P], ident[:])
                 nc.scalar.copy(placed_turned[:, h * (TBLOCKS // 2) : (h + 1) * (TBLOCKS // 2), :].rearrange("p c d -> p (c d)"), forth[:])
             for h in range(2):
-                back = bank((5, 0)[h], "sum%d_%d" % (m, h))
+                back = bank((0, 1)[h], "sum%d_%d" % (m, h))
                 for c in range(TBLOCKS // 2):
                     b = h * (TBLOCKS // 2) + c
                     nc.tensor.matmul(back[:, c * P : (c + 1) * P], faded[:, b, m * P : (m + 1) * P], ident[:], start=True, stop=False, is_transpose=True)
@@ -246,12 +268,15 @@ def tile_attend_bpairquota_x_kernel(tc, taba, tabb_words, tabb_scales, reserve, 
                 nc.scalar.copy(result[m][:, h * BANK : (h + 1) * BANK], back[:])
                 store(nc.scalar, m, h * BANK, (h + 1) * BANK)
 
-        for a in range(HALVES):
-            for m in range(2):
-                scatter(m, a * P, (a + 1) * P, gx_front[a][:, m, :])
-        add_on_tensor(0)
-        scatter(2, 0, I, gx_rear[:, 0, :])
+        for h in range(2):
+            fade_old(h)
+        late = second_product(1, (0, 1, 2, 3), 6)
+        place(late, 0, 0, 1, "gx_x")
+        add_on_gpsimd(0)
+        place(late, 1, 1, 1, "gx_y")
         add_on_tensor(1)
+        place(rear, 1, 3, 0, "gx_x")
+        place(late, 2, 2, 1, "gx_y")
         add_on_vector(2, (1, 1))
-        scatter(3, 0, I, gx_rear[:, 1, :])
+        place(late, 3, 3, 1, "gx_y")
         add_on_vector(3, (1, 2))

@@ -50,16 +50,11 @@ def tile_attend_bpairquota_x_kernel(tc, taba, tabb_words, tabb_scales, reserve, 
         for q in range(4):
             nc.scalar.dma_start(scale_table[32 * q : 32 * q + 32, :].bitcast(I32), tabb_scales[:, 4 * q : 4 * q + 4, :].bitcast(I32).to_broadcast([8, 4, U // 4]))
         warm = sb.tile([P, 8], F32, name="warm")
-        nc.vector.memset(warm[:], 0.0)
+        nc.gpsimd.memset(warm[:], 0.0)
         warm_out = sb.tile([P, 8], F32, name="warm_out")
         nc.scalar.activation(warm_out[:], warm[:], ACT.Sigmoid)
-        nc.gpsimd.dma_start(vector_rows[FADE_ROW:JS_ROW, :], fade.rearrange("o (b p) -> o b p", p=P).to_broadcast([8, TBLOCKS, P]))
-        nc.gpsimd.dma_start(vector_rows[JS_ROW:RESERVE_ROW, :], js.rearrange("o (b p) -> o b p", p=P).to_broadcast([8, J // P, P]))
-        nc.gpsimd.dma_start(vector_rows[RESERVE_ROW:P, :], reserve.rearrange("(a p) o -> o a p", p=P).to_broadcast([16, HALVES, P]))
-        stakes = sb.tile([P, HALVES, G], F32, name="stakes")
-        nc.gpsimd.dma_start(stakes[:], stake.rearrange("(a p) g -> p a g", p=P))
         for m in range(PLANES):
-            (nc.vector if m < 2 else nc.gpsimd).memset(placed[m][:].bitcast(I32), 0)
+            nc.gpsimd.memset(placed[m][:], 0.0)
         word_table = sb.tile([P, U], U16, name="word_table")
         nc.sync.dma_start(word_table[:].bitcast(I32), tabb_words[0].bitcast(I32))
         list_a = lists.tile([P, I // 16], U16, name="list_a")
@@ -68,8 +63,13 @@ def tile_attend_bpairquota_x_kernel(tc, taba, tabb_words, tabb_scales, reserve, 
         a_table = [sb.tile([P, T], F32, name="a_table%d" % r) for r in range(PACK)]
         for r in range(PACK):
             nc.sync.dma_start(a_table[r][:], a_rows[:, r, :])
-        b_table = [sb.tile([P, U], F32, name="b_table%d" % m, tag="b_table%d" % m) for m in range(PLANES)]
+        nc.sync.dma_start(vector_rows[FADE_ROW:JS_ROW, :], fade.rearrange("o (b p) -> o b p", p=P).to_broadcast([8, TBLOCKS, P]))
+        nc.sync.dma_start(vector_rows[JS_ROW:RESERVE_ROW, :], js.rearrange("o (b p) -> o b p", p=P).to_broadcast([8, J // P, P]))
+        nc.sync.dma_start(vector_rows[RESERVE_ROW:P, :], reserve.rearrange("(a p) o -> o a p", p=P).to_broadcast([16, HALVES, P]))
+        b_table = [sb.tile([P, U], F32, name="b_table%d" % m) for m in range(PLANES)]
         nc.sync.dma_start(b_table[0][:], brows[0:P, :])
+        stakes = sb.tile([P, HALVES, G], F32, name="stakes")
+        nc.sync.dma_start(stakes[:], stake.rearrange("(a p) g -> p a g", p=P))
         for m in range(1, PLANES):
             nc.sync.dma_start(b_table[m][:], brows[m * P : (m + 1) * P, :])
         old_half = [sb.tile([P, PLANES, BANK], F32, name="old_half%d" % h) for h in range(2)]
@@ -81,11 +81,7 @@ def tile_attend_bpairquota_x_kernel(tc, taba, tabb_words, tabb_scales, reserve, 
         b_words = sb.tile([P, J], U16, name="b_words", align_bytes=64)
         nc.vector.tensor_copy(b_words[:], word_table[:].indirect(list_b[:]))
         a_woven = sb.tile([P, I, PACK], BF16, name="a_woven", align_bytes=64)
-        a_picked = sb.tile([P, 2, I], BF16, name="a_picked")
-        for r in range(2):
-            nc.vector.tensor_copy(a_picked[:, r, :], a_table[r][:].indirect(list_a[:]))
-        nc.scalar.copy(a_woven[:, :, 0:2], a_picked[:].rearrange("p r i -> p i r"))
-        for r in range(2, PACK):
+        for r in range(PACK):
             nc.vector.tensor_copy(a_woven[:, :, r], a_table[r][:].indirect(list_a[:]))
         a_codes = sb.tile([P, I], U32, name="a_codes", align_bytes=64)
         a_scales = sb.tile([P, I], U8, name="a_scales", align_bytes=64)
@@ -105,11 +101,11 @@ def tile_attend_bpairquota_x_kernel(tc, taba, tabb_words, tabb_scales, reserve, 
 
         turned = bank(2, "turned")
         nc.tensor.transpose(turned[:, 0:P], vector_rows[:], ident[:])
-        columns = sb.tile([P, P], F32, name="columns")
-        nc.scalar.copy(columns[:], turned[:, 0:P])
+        columns = sb.tile([P, 4, TBLOCKS], F32, name="columns")
+        nc.vector.tensor_copy(columns[:], turned[:, 0:P].rearrange("p (q c) -> p q c", q=4)[:, :, 0:TBLOCKS])
         js_wide = bank(3, "js_wide")
         for b in range(J // P):
-            nc.tensor.transpose(js_wide[:, b * P : (b + 1) * P], columns[:, JS_ROW + b : JS_ROW + b + 1].to_broadcast([P, P]), ident[:])
+            nc.tensor.transpose(js_wide[:, b * P : (b + 1) * P], columns[:, JS_ROW // 32, b : b + 1].to_broadcast([P, P]), ident[:])
 
         bt_woven = sb.tile([P, D, PACK], BF16, name="bt_woven", tag="log_low1", align_bytes=64)
         bt_scales = sb.tile([P, D], U8, name="bt_scales", align_bytes=64)
@@ -147,7 +143,7 @@ def tile_attend_bpairquota_x_kernel(tc, taba, tabb_words, tabb_scales, reserve, 
 
         def sums(a):
             nc.vector.tensor_reduce(group_sum[a][:], soft[a][:].rearrange("p (g k) -> p g k", k=GROUP), AXIS.X, ALU.add)
-            nc.vector.tensor_scalar(den[a][:, G : G + 1], row_sum[a][:], columns[:, RESERVE_ROW + a : RESERVE_ROW + a + 1], None, ALU.add)
+            nc.vector.tensor_scalar(den[a][:, G : G + 1], row_sum[a][:], columns[:, RESERVE_ROW // 32, a : a + 1], None, ALU.add)
 
         def denominators(a):
             nc.vector.tensor_scalar(den[a][:, 0:G], group_sum[a][:], 64.0, den[a][:, G : G + 1], ALU.mult, ALU.add)
@@ -179,7 +175,7 @@ def tile_attend_bpairquota_x_kernel(tc, taba, tabb_words, tabb_scales, reserve, 
                 old_turned = bank((4, 5, 0, 1)[c], "old_turned%d" % b)
                 for m in range(PLANES):
                     nc.tensor.transpose(old_turned[:, m * P : (m + 1) * P], old_half[h][:, m, c * P : (c + 1) * P], ident[:])
-                nc.scalar.activation(faded[:, b, :], old_turned[:], ACT.Copy, scale=columns[:, FADE_ROW + b : FADE_ROW + b + 1])
+                nc.scalar.activation(faded[:, b, :], old_turned[:], ACT.Copy, scale=columns[:, FADE_ROW // 32, b : b + 1])
 
         for a in range(HALVES):
             softplus(a)
@@ -231,7 +227,7 @@ def tile_attend_bpairquota_x_kernel(tc, taba, tabb_words, tabb_scales, reserve, 
 
         def add_on_vector(m, pieces):
             for h in range(2):
-                back = bank((2, 3, 7, 4)[2 * (m - 2) + h], "back%d_%d" % (m, h))
+                back = bank((2, 3, 0, 1, 7, 2)[2 * (m - 1) + h], "back%d_%d" % (m, h))
                 for c in range(TBLOCKS // 2):
                     nc.tensor.transpose(back[:, c * P : (c + 1) * P], faded[:, h * (TBLOCKS // 2) + c, m * P : (m + 1) * P], ident[:])
                 width = BANK // pieces[h]
@@ -239,17 +235,6 @@ def tile_attend_bpairquota_x_kernel(tc, taba, tabb_words, tabb_scales, reserve, 
                     t0 = h * BANK + c0
                     nc.vector.tensor_tensor(result[m][:, t0 : t0 + width], back[:, c0 : c0 + width], placed[m][:, t0 : t0 + width], ALU.add)
                     store(nc.sync, m, t0, t0 + width)
-
-        def add_on_gpsimd(m):
-            faded_plane = sb.tile([P, T], F32, name="faded_plane%d" % m)
-            for h in range(2):
-                cols = slice(h * BANK, (h + 1) * BANK)
-                back = bank((2, 3)[h], "back%d_%d" % (m, h))
-                for c in range(TBLOCKS // 2):
-                    nc.tensor.transpose(back[:, c * P : (c + 1) * P], faded[:, h * (TBLOCKS // 2) + c, m * P : (m + 1) * P], ident[:])
-                nc.scalar.copy(faded_plane[:, cols], back[:])
-                nc.gpsimd.tensor_tensor(result[m][:, cols], faded_plane[:, cols], placed[m][:, cols], ALU.add)
-                store(nc.sync, m, h * BANK, (h + 1) * BANK)
 
         def add_on_tensor(m):
             placed_turned = sb.tile([P, TBLOCKS, P], F32, name="placed_turned%d" % m)
@@ -260,7 +245,7 @@ def tile_attend_bpairquota_x_kernel(tc, taba, tabb_words, tabb_scales, reserve, 
                     nc.tensor.transpose(forth[:, c * P : (c + 1) * P], placed[m][:, b * P : (b + 1) * P], ident[:])
                 nc.scalar.copy(placed_turned[:, h * (TBLOCKS // 2) : (h + 1) * (TBLOCKS // 2), :].rearrange("p c d -> p (c d)"), forth[:])
             for h in range(2):
-                back = bank((0, 1)[h], "sum%d_%d" % (m, h))
+                back = bank((4, 5)[h], "sum%d_%d" % (m, h))
                 for c in range(TBLOCKS // 2):
                     b = h * (TBLOCKS // 2) + c
                     nc.tensor.matmul(back[:, c * P : (c + 1) * P], faded[:, b, m * P : (m + 1) * P], ident[:], start=True, stop=False, is_transpose=True)
@@ -272,9 +257,9 @@ def tile_attend_bpairquota_x_kernel(tc, taba, tabb_words, tabb_scales, reserve, 
             fade_old(h)
         late = second_product(1, (0, 1, 2, 3), 6)
         place(late, 0, 0, 1, "gx_x")
-        add_on_gpsimd(0)
+        add_on_tensor(0)
         place(late, 1, 1, 1, "gx_y")
-        add_on_tensor(1)
+        add_on_vector(1, (1, 1))
         place(rear, 1, 3, 0, "gx_x")
         place(late, 2, 2, 1, "gx_y")
         add_on_vector(2, (1, 1))

@@ -49,10 +49,11 @@ def tile_attend_bpairquota_x_kernel(tc, taba, tabb_words, tabb_scales, reserve, 
         nc.sync.dma_start(list_b[:], offs2)
         for q in range(4):
             nc.scalar.dma_start(scale_table[32 * q : 32 * q + 32, :].bitcast(I32), tabb_scales[:, 4 * q : 4 * q + 4, :].bitcast(I32).to_broadcast([8, 4, U // 4]))
-        warm = sb.tile([P, 8], F32, name="warm")
-        nc.gpsimd.memset(warm[:], 0.0)
-        warm_out = sb.tile([P, 8], F32, name="warm_out")
-        nc.scalar.activation(warm_out[:], warm[:], ACT.Sigmoid)
+        nc.scalar.dma_start(vector_rows[FADE_ROW:JS_ROW, :], fade.rearrange("o (b p) -> o b p", p=P).to_broadcast([8, TBLOCKS, P]))
+        nc.scalar.dma_start(vector_rows[JS_ROW:RESERVE_ROW, :], js.rearrange("o (b p) -> o b p", p=P).to_broadcast([8, J // P, P]))
+        nc.scalar.dma_start(vector_rows[RESERVE_ROW:P, :], reserve.rearrange("(a p) o -> o a p", p=P).to_broadcast([16, HALVES, P]))
+        stakes = sb.tile([P, HALVES, G], F32, name="stakes")
+        nc.scalar.dma_start(stakes[:], stake.rearrange("(a p) g -> p a g", p=P))
         for m in range(PLANES):
             nc.gpsimd.memset(placed[m][:], 0.0)
         word_table = sb.tile([P, U], U16, name="word_table")
@@ -60,16 +61,15 @@ def tile_attend_bpairquota_x_kernel(tc, taba, tabb_words, tabb_scales, reserve, 
         list_a = lists.tile([P, I // 16], U16, name="list_a")
         nc.sync.dma_start(list_a[:], offs)
         a_rows = taba.rearrange("(p r) t -> p r t", r=PACK)
-        a_table = [sb.tile([P, T], F32, name="a_table%d" % r) for r in range(PACK)]
-        for r in range(PACK):
-            nc.sync.dma_start(a_table[r][:], a_rows[:, r, :])
-        nc.sync.dma_start(vector_rows[FADE_ROW:JS_ROW, :], fade.rearrange("o (b p) -> o b p", p=P).to_broadcast([8, TBLOCKS, P]))
-        nc.sync.dma_start(vector_rows[JS_ROW:RESERVE_ROW, :], js.rearrange("o (b p) -> o b p", p=P).to_broadcast([8, J // P, P]))
-        nc.sync.dma_start(vector_rows[RESERVE_ROW:P, :], reserve.rearrange("(a p) o -> o a p", p=P).to_broadcast([16, HALVES, P]))
+        a_first = sb.tile([P, 2, T], F32, name="a_first")
+        nc.sync.dma_start(a_first[:], a_rows[:, 0:2, :])
+        a_table = [a_first[:, 0, :], a_first[:, 1, :]]
+        for r in range(2, PACK):
+            a_plane = sb.tile([P, T], F32, name="a_plane%d" % r)
+            nc.sync.dma_start(a_plane[:], a_rows[:, r, :])
+            a_table.append(a_plane[:])
         b_table = [sb.tile([P, U], F32, name="b_table%d" % m) for m in range(PLANES)]
         nc.sync.dma_start(b_table[0][:], brows[0:P, :])
-        stakes = sb.tile([P, HALVES, G], F32, name="stakes")
-        nc.sync.dma_start(stakes[:], stake.rearrange("(a p) g -> p a g", p=P))
         for m in range(1, PLANES):
             nc.sync.dma_start(b_table[m][:], brows[m * P : (m + 1) * P, :])
         old_half = [sb.tile([P, PLANES, BANK], F32, name="old_half%d" % h) for h in range(2)]
@@ -82,7 +82,7 @@ def tile_attend_bpairquota_x_kernel(tc, taba, tabb_words, tabb_scales, reserve, 
         nc.vector.tensor_copy(b_words[:], word_table[:].indirect(list_b[:]))
         a_woven = sb.tile([P, I, PACK], BF16, name="a_woven", align_bytes=64)
         for r in range(PACK):
-            nc.vector.tensor_copy(a_woven[:, :, r], a_table[r][:].indirect(list_a[:]))
+            nc.vector.tensor_copy(a_woven[:, :, r], a_table[r].indirect(list_a[:]))
         a_codes = sb.tile([P, I], U32, name="a_codes", align_bytes=64)
         a_scales = sb.tile([P, I], U8, name="a_scales", align_bytes=64)
         nc.vector.quantize_mx(out=a_codes[:].bitcast(FP8X4), scales=a_scales[:], in_=a_woven[:].rearrange("p i r -> p (i r)"))
@@ -102,7 +102,7 @@ def tile_attend_bpairquota_x_kernel(tc, taba, tabb_words, tabb_scales, reserve, 
         turned = bank(2, "turned")
         nc.tensor.transpose(turned[:, 0:P], vector_rows[:], ident[:])
         columns = sb.tile([P, 4, TBLOCKS], F32, name="columns")
-        nc.vector.tensor_copy(columns[:], turned[:, 0:P].rearrange("p (q c) -> p q c", q=4)[:, :, 0:TBLOCKS])
+        nc.scalar.copy(columns[:], turned[:, 0:P].rearrange("p (q c) -> p q c", q=4)[:, :, 0:TBLOCKS])
         js_wide = bank(3, "js_wide")
         for b in range(J // P):
             nc.tensor.transpose(js_wide[:, b * P : (b + 1) * P], columns[:, JS_ROW // 32, b : b + 1].to_broadcast([P, P]), ident[:])

from contextlib import ExitStack

import concourse.mybir as mybir
from concourse.masks import make_identity

D, T, U, I, J, G = 512, 1024, 1024, 256, 512, 64
FLOPS = 2 * D * I * J * 2

F32 = mybir.dt.float32
BF16 = mybir.dt.bfloat16
I32 = mybir.dt.int32
U32 = mybir.dt.uint32
U16 = mybir.dt.uint16
U8 = mybir.dt.uint8
FP8X4 = mybir.dt.float8_e4m3fn_x4
FP4X4 = mybir.dt.float4_e2m1fn_x4
ALU = mybir.AluOpType
ACT = mybir.ActivationFunctionType
AXIS = mybir.AxisListType

P = 128
PACK = 4
HALVES = I // P
PLANES = D // P
TBLOCKS = T // P
GROUP = J // G
BANK = 512
TINY = 2.0 ** -60
FADE_ROW, JS_ROW, RESERVE_ROW = 0, 64, 96


def tile_attend_bpairquota_x_kernel(tc, taba, tabb_words, tabb_scales, reserve, stake, js, brows, old, fade, offs, offs2, out):
    nc = tc.nc
    with ExitStack() as ctx:
        lists = ctx.enter_context(tc.tile_pool(name="lists", bufs=1))
        sb = ctx.enter_context(tc.tile_pool(name="sb", bufs=1))
        ps = ctx.enter_context(tc.psum_pool(name="ps", bufs=1))

        def bank(n, name):
            return ps.tile([P, BANK], F32, name=name, tag="bank%d" % n)

        scale_table = sb.tile([P, U], U8, name="scale_table")
        vector_rows = sb.tile([P, P], F32, name="vector_rows")
        placed = [sb.tile([P, T], F32, name="placed%d" % m) for m in range(PLANES)]
        ident = sb.tile([P, P], F32, name="ident")
        make_identity(nc, ident[:])

        list_b = lists.tile([P, J // 16], U16, name="list_b")
        nc.sync.dma_start(list_b[:], offs2)
        for q in range(4):
            nc.scalar.dma_start(scale_table[32 * q : 32 * q + 32, :].bitcast(I32), tabb_scales[:, 4 * q : 4 * q + 4, :].bitcast(I32).to_broadcast([8, 4, U // 4]))
        nc.scalar.dma_start(vector_rows[FADE_ROW:JS_ROW, :], fade.rearrange("o (b p) -> o b p", p=P).to_broadcast([8, TBLOCKS, P]))
        nc.scalar.dma_start(vector_rows[JS_ROW:RESERVE_ROW, :], js.rearrange("o (b p) -> o b p", p=P).to_broadcast([8, J // P, P]))
        nc.scalar.dma_start(vector_rows[RESERVE_ROW:P, :], reserve.rearrange("(a p) o -> o a p", p=P).to_broadcast([16, HALVES, P]))
        stakes = sb.tile([P, HALVES, G], F32, name="stakes")
        nc.scalar.dma_start(stakes[:], stake.rearrange("(a p) g -> p a g", p=P))
        for m in range(PLANES):
            nc.gpsimd.memset(placed[m][:], 0.0)
        word_table = sb.tile([P, U], U16, name="word_table")
        nc.sync.dma_start(word_table[:].bitcast(I32), tabb_words[0].bitcast(I32))
        list_a = lists.tile([P, I // 16], U16, name="list_a")
        nc.sync.dma_start(list_a[:], offs)
        a_rows = taba.rearrange("(p r) t -> p r t", r=PACK)
        a_first = sb.tile([P, 2, T], F32, name="a_first")
        nc.sync.dma_start(a_first[:], a_rows[:, 0:2, :])
        a_table = [a_first[:, 0, :], a_first[:, 1, :]]
        for r in range(2, PACK):
            a_plane = sb.tile([P, T], F32, name="a_plane%d" % r)
            nc.sync.dma_start(a_plane[:], a_rows[:, r, :])
            a_table.append(a_plane[:])
        b_table = [sb.tile([P, U], F32, name="b_table%d" % m) for m in range(PLANES)]
        nc.sync.dma_start(b_table[0][:], brows[0:P, :])
        for m in range(1, PLANES):
            nc.sync.dma_start(b_table[m][:], brows[m * P : (m + 1) * P, :])
        old_half = [sb.tile([P, PLANES, BANK], F32, name="old_half%d" % h) for h in range(2)]
        for h in range(2):
            nc.sync.dma_start(old_half[h][:], old[:, h * BANK : (h + 1) * BANK].rearrange("(m p) t -> p m t", p=P))

        b_scales = sb.tile([P, J], U8, name="b_scales", align_bytes=64)
        nc.vector.tensor_copy(b_scales[:], scale_table[:].indirect(list_b[:]))
        b_words = sb.tile([P, J], U16, name="b_words", align_bytes=64)
        nc.vector.tensor_copy(b_words[:], word_table[:].indirect(list_b[:]))
        a_woven = sb.tile([P, I, PACK], BF16, name="a_woven", align_bytes=64)
        for r in range(PACK):
            nc.vector.tensor_copy(a_woven[:, :, r], a_table[r].indirect(list_a[:]))
        a_codes = sb.tile([P, I], U32, name="a_codes", align_bytes=64)
        a_scales = sb.tile([P, I], U8, name="a_scales", align_bytes=64)
        nc.vector.quantize_mx(out=a_codes[:].bitcast(FP8X4), scales=a_scales[:], in_=a_woven[:].rearrange("p i r -> p (i r)"))

        score = [bank(a, "score%d" % a) for a in range(HALVES)]
        for a in range(HALVES):
            nc.tensor.matmul_mx(out=score[a][:], lhsT=a_codes[:, a * P : (a + 1) * P].bitcast(FP8X4), lhsT_scale=a_scales[:, a * P : (a + 1) * P],
                                rhs=b_words[:].bitcast(FP4X4), rhs_scale=b_scales[:], start=True, stop=True)
        low = [sb.tile([P, J], F32, name="low%d" % a, tag="low%d" % a, align_bytes=64) for a in range(HALVES)]
        sig = [sb.tile([P, J], F32, name="sig%d" % a, tag="low%d" % a, align_bytes=64) for a in range(HALVES)]
        log_low = [sb.tile([P, J], F32, name="log_low%d" % a, tag="log_low%d" % a, align_bytes=64) for a in range(HALVES)]
        for a in range(HALVES):
            nc.scalar.activation(low[a][:], score[a][:], ACT.Sigmoid, scale=-1.0)
        for a in range(HALVES):
            nc.scalar.activation(log_low[a][:], low[a][:], ACT.Ln, bias=TINY)

        turned = bank(2, "turned")
        nc.tensor.transpose(turned[:, 0:P], vector_rows[:], ident[:])
        columns = sb.tile([P, 4, TBLOCKS], F32, name="columns")
        nc.scalar.copy(columns[:], turned[:, 0:P].rearrange("p (q c) -> p q c", q=4)[:, :, 0:TBLOCKS])
        js_wide = bank(3, "js_wide")
        for b in range(J // P):
            nc.tensor.transpose(js_wide[:, b * P : (b + 1) * P], columns[:, JS_ROW // 32, b : b + 1].to_broadcast([P, P]), ident[:])

        bt_woven = sb.tile([P, D, PACK], BF16, name="bt_woven", tag="log_low1", align_bytes=64)
        bt_scales = sb.tile([P, D], U8, name="bt_scales", align_bytes=64)
        bt_turned = [bank(4 + pair, "bt_turned%d" % pair) for pair in range(PLANES // 2)]
        for pair in range(PLANES // 2):
            for k in range(2):
                m = 2 * pair + k
                b_picked = sb.tile([P, J], BF16, name="b_picked%d" % m)
                nc.vector.tensor_copy(b_picked[:], b_table[m][:].indirect(list_b[:]))
                words = b_picked[:].bitcast(F32)
                for u in range(2):
                    nc.tensor.transpose(bt_turned[pair][:, (2 * k + u) * P : (2 * k + u + 1) * P], words[:, u : J // 2 : 2], ident[:])

        soft = [sb.tile([P, J], F32, name="soft%d" % a) for a in range(HALVES)]
        row_sum = [sb.tile([P, 1], F32, name="row_sum%d" % a) for a in range(HALVES)]
        group_sum = [sb.tile([P, G], F32, name="group_sum%d" % a, tag=("sig_js", "group_sum1")[a]) for a in range(HALVES)]
        sig_js = [sb.tile([P, J], F32, name="sig_js%d" % a, tag="sig_js") for a in range(HALVES)]
        den = [sb.tile([P, G + 1], F32, name="den%d" % a) for a in range(HALVES)]
        e1 = [sb.tile([P, G, 1], F32, name="e1_%d" % a, tag="e1_%d" % a) for a in range(HALVES)]
        inv = [sb.tile([P, G + 1], F32, name="inv%d" % a, tag=("inv0", "e1_0")[a]) for a in range(HALVES)]
        staked = [sb.tile([P, G], F32, name="staked%d" % a, tag="staked%d" % a, align_bytes=64) for a in range(HALVES)]
        bt_codes = sb.tile([P, D], U32, name="bt_codes", tag="staked0", align_bytes=64)
        terms = [sb.tile([P, G], F32, name="terms%d" % a) for a in range(HALVES)]
        minus_dz = [sb.tile([P, 1], F32, name="minus_dz%d" % a) for a in range(HALVES)]
        gs = [sb.tile([P, J], BF16, name="gs%d" % a) for a in range(HALVES)]
        gt_codes = sb.tile([P, I], U32, name="gt_codes", align_bytes=64)
        gt_scales = sb.tile([P, I], U8, name="gt_scales", align_bytes=64)
        gt_woven = [sb.tile([P, P, PACK], BF16, name="gt_woven%d" % a, align_bytes=64) for a in range(HALVES)]

        def scaled_sigmoid(a):
            nc.vector.tensor_tensor(sig_js[a][:], sig[a][:], js_wide[:], ALU.mult)

        def softplus(a):
            nc.vector.scalar_tensor_tensor(soft[a][:], log_low[a][:], -1.0, score[a][:], ALU.mult, ALU.max, accum_out=row_sum[a][:])

        def sums(a):
            nc.vector.tensor_reduce(group_sum[a][:], soft[a][:].rearrange("p (g k) -> p g k", k=GROUP), AXIS.X, ALU.add)
            nc.vector.tensor_scalar(den[a][:, G : G + 1], row_sum[a][:], columns[:, RESERVE_ROW // 32, a : a + 1], None, ALU.add)

        def denominators(a):
            nc.vector.tensor_scalar(den[a][:, 0:G], group_sum[a][:], 64.0, den[a][:, G : G + 1], ALU.mult, ALU.add)
            nc.vector.scalar_tensor_tensor(staked[a][:], group_sum[a][:], 64.0, stakes[:, a, :], ALU.mult, ALU.mult)

        def inverses(a):
            nc.vector.reciprocal(inv[a][:], den[a][:])

        def group_terms(a):
            nc.vector.scalar_tensor_tensor(e1[a][:, :, 0], inv[a][:, 0:G], 64.0, stakes[:, a, :], ALU.mult, ALU.mult)

        def row_term(a):
            nc.vector.scalar_tensor_tensor(terms[a][:], inv[a][:, 0:G], inv[a][:, G : G + 1], staked[a][:], ALU.mult, ALU.mult, accum_out=minus_dz[a][:])

        def gradient(a):
            nc.vector.scalar_tensor_tensor(gs[a][:].rearrange("p (g k) -> p g k", k=GROUP), e1[a][:].to_broadcast([P, G, GROUP]), minus_dz[a][:],
                                           sig_js[a][:].rearrange("p (g k) -> p g k", k=GROUP), ALU.subtract, ALU.mult)
            gt_turned = bank((6, 7)[a], "gt_turned%d" % a)
            words = gs[a][:].bitcast(F32)
            for u in range(2):
                nc.tensor.transpose(gt_turned[:, u * P : (u + 1) * P], words[:, u : J // 2 : 2], ident[:])
            nc.scalar.copy(gt_woven[a][:].bitcast(F32), gt_turned[:, 0 : 2 * P].rearrange("p (u i) -> p i u", u=2))

        faded = sb.tile([P, TBLOCKS, D], F32, name="faded")

        def fade_old(h):
            for c in range(TBLOCKS // 2):
                b = h * (TBLOCKS // 2) + c
                old_turned = bank((4, 5, 0, 1)[c], "old_turned%d" % b)
                for m in range(PLANES):
                    nc.tensor.transpose(old_turned[:, m * P : (m + 1) * P], old_half[h][:, m, c * P : (c + 1) * P], ident[:])
                nc.scalar.activation(faded[:, b, :], old_turned[:], ACT.Copy, scale=columns[:, FADE_ROW // 32, b : b + 1])

        for a in range(HALVES):
            softplus(a)
        for a in range(HALVES):
            nc.scalar.activation(sig[a][:], score[a][:], ACT.Sigmoid)
        for pair in range(PLANES // 2):
            nc.scalar.copy(bt_woven[:, pair * 2 * P : (pair + 1) * 2 * P, :].bitcast(F32).rearrange("p (k d) u -> p k d u", k=2),
                           bt_turned[pair][:].rearrange("p (k u d) -> p k d u", k=2, u=2))
        for a in range(HALVES):
            sums(a)
            denominators(a)
            inverses(a)
            row_term(a)
            group_terms(a)
            scaled_sigmoid(a)
            gradient(a)
            if a == 0:
                nc.vector.quantize_mx(out=bt_codes[:].bitcast(FP8X4), scales=bt_scales[:], in_=bt_woven[:].rearrange("p d r -> p (d r)"))

        def quantise_gt(a):
            cols = slice(a * P, (a + 1) * P)
            nc.vector.quantize_mx(out=gt_codes[:, cols].bitcast(FP8X4), scales=gt_scales[:, cols], in_=gt_woven[a][:].rearrange("p i r -> p (i r)"))

        def second_product(a, planes, n):
            cols = slice(a * P, (a + 1) * P)
            product = bank(n, "product%d_%d" % (a, planes[0]))
            for k, m in enumerate(planes):
                nc.tensor.matmul_mx(out=product[:, k * P : (k + 1) * P], lhsT=bt_codes[:, m * P : (m + 1) * P].bitcast(FP8X4), lhsT_scale=bt_scales[:, m * P : (m + 1) * P],
                                    rhs=gt_codes[:, cols].bitcast(FP8X4), rhs_scale=gt_scales[:, cols], start=True, stop=True)
            return product

        quantise_gt(0)
        quantise_gt(1)
        def place(product, k, m, a, tag):
            values = sb.tile([P, P], F32, name="gx%d_%d" % (m, a), tag=tag)
            nc.scalar.copy(values[:], product[:, k * P : (k + 1) * P])
            nc.vector.tensor_copy(placed[m][:].indirect(list_a[:, a * (P // 16) : (a + 1) * (P // 16)]), values[:])

        front = second_product(0, (0, 1), 2)
        place(front, 0, 0, 0, "gx_0")
        place(front, 1, 1, 0, "gx_1")
        rear = second_product(0, (2, 3), 7)
        place(rear, 0, 2, 0, "gx_2")

        result = [sb.tile([P, T], F32, name="result%d" % m) for m in range(PLANES)]

        def store(queue, m, c0, c1):
            queue.dma_start(out[m * P : (m + 1) * P, c0:c1], result[m][:, c0:c1])

        def add_on_vector(m, pieces):
            for h in range(2):
                back = bank((2, 3, 0, 1, 7, 2)[2 * (m - 1) + h], "back%d_%d" % (m, h))
                for c in range(TBLOCKS // 2):
                    nc.tensor.transpose(back[:, c * P : (c + 1) * P], faded[:, h * (TBLOCKS // 2) + c, m * P : (m + 1) * P], ident[:])
                width = BANK // pieces[h]
                for c0 in range(0, BANK, width):
                    t0 = h * BANK + c0
                    nc.vector.tensor_tensor(result[m][:, t0 : t0 + width], back[:, c0 : c0 + width], placed[m][:, t0 : t0 + width], ALU.add)
                    store(nc.sync, m, t0, t0 + width)

        def add_on_tensor(m):
            placed_turned = sb.tile([P, TBLOCKS, P], F32, name="placed_turned%d" % m)
            for h in range(2):
                forth = bank((4, 5)[h], "forth%d_%d" % (m, h))
                for c in range(TBLOCKS // 2):
                    b = h * (TBLOCKS // 2) + c
                    nc.tensor.transpose(forth[:, c * P : (c + 1) * P], placed[m][:, b * P : (b + 1) * P], ident[:])
                nc.scalar.copy(placed_turned[:, h * (TBLOCKS // 2) : (h + 1) * (TBLOCKS // 2), :].rearrange("p c d -> p (c d)"), forth[:])
            for h in range(2):
                back = bank((4, 5)[h], "sum%d_%d" % (m, h))
                for c in range(TBLOCKS // 2):
                    b = h * (TBLOCKS // 2) + c
                    nc.tensor.matmul(back[:, c * P : (c + 1) * P], faded[:, b, m * P : (m + 1) * P], ident[:], start=True, stop=False, is_transpose=True)
                    nc.tensor.matmul(back[:, c * P : (c + 1) * P], placed_turned[:, b, :], ident[:], start=False, stop=True, is_transpose=True)
                nc.scalar.copy(result[m][:, h * BANK : (h + 1) * BANK], back[:])
                store(nc.scalar, m, h * BANK, (h + 1) * BANK)

        for h in range(2):
            fade_old(h)
        late = second_product(1, (0, 1, 2, 3), 6)
        place(late, 0, 0, 1, "gx_x")
        add_on_tensor(0)
        place(late, 1, 1, 1, "gx_y")
        add_on_vector(1, (1, 1))
        place(rear, 1, 3, 0, "gx_x")
        place(late, 2, 2, 1, "gx_y")
        add_on_vector(2, (1, 1))
        place(late, 3, 3, 1, "gx_y")
        add_on_vector(3, (1, 2))
